import numpy as np
import ml_dtypes


def mxq(x, axis, fmt="e4m3"):
    dtype, down = {"e4m3": (ml_dtypes.float8_e4m3fn, 7), "e5m2": (ml_dtypes.float8_e5m2, 14)}[fmt]
    v = np.moveaxis(np.asarray(x, np.float32).astype(ml_dtypes.bfloat16).astype(np.float64), axis, -1)
    blocks = v.reshape(v.shape[:-1] + (-1, 32))
    amax = np.abs(blocks).max(-1, keepdims=True)
    byte = np.maximum(np.where(amax > 0, np.frexp(amax)[1] - 1 + 127, 0) - down, 1)
    scale = np.exp2(byte - 127.0)
    codes = (blocks / scale).astype(np.float32).astype(dtype).astype(np.float64)
    return np.moveaxis((codes * scale).reshape(v.shape), -1, axis)


WIDE = False


def mx_kscale(k):
    if not WIDE:
        return np.ones(k)
    levels = np.array([10, -10, 5, -5, 0])
    if k % 512:
        return np.exp2(np.random.permutation(np.resize(levels, k // 32))).repeat(32)
    a = np.empty((k // 512, 16))
    for p in range(k // 512):
        a[p, :8] = np.random.permutation(np.resize(levels, 8))
        for g in range(8):
            far = levels[np.abs(levels - a[p, g]) >= 10]
            a[p, g + 8] = far[np.random.randint(len(far))]
    return np.exp2(a.ravel()).repeat(32)


BF16 = ml_dtypes.bfloat16


def bf(x):
    return np.asarray(x, np.float32).astype(BF16)


def f64(x):
    return np.asarray(x).astype(np.float64)


D, F, N = 2048, 128, 2048

ALPHA = 0.5


def draw0():
    s = mx_kscale(N)
    t = mx_kscale(N)
    c = 1.0 / np.sqrt(N)
    return {
        "w0": bf(np.random.standard_normal((D, F)) * 0.5),
        "coef": bf(np.random.standard_normal((N, N)) * c * s[None, :]),
        "g": bf((1.0 + 0.1 * np.random.standard_normal(N)) * t),
        "uc": bf(np.random.standard_normal((D, N)) * c / t[None, :]),
        "us": bf(np.random.standard_normal((D, N)) * c / t[None, :]),
        "vc": bf(np.random.standard_normal((N, F)) / s[:, None]),
        "vs": bf(np.random.standard_normal((N, F)) / s[:, None]),
    }


def core(w0, coef, g, uc, us, vc, vs):
    cq = mxq(f64(coef), 1, "e4m3")
    rc = cq @ mxq(f64(vc), 0, "e4m3")
    rs = cq @ mxq(f64(vs), 0, "e4m3")
    gain = f64(g)[:, None]
    zc = gain * rc
    zs = gain * rs
    pc = mxq(f64(uc), 1, "e4m3") @ mxq(zc, 0, "e4m3")
    ps = mxq(f64(us), 1, "e4m3") @ mxq(zs, 0, "e4m3")
    return f64(w0) + ALPHA * (pc - ps)


def e4m3fn_bytes(y):
    return np.clip(np.asarray(y, np.float64), -448.0, 448.0).astype(np.float32).astype(ml_dtypes.float8_e4m3fn).view(np.uint8)


def e4m3fn_values(b):
    return np.asarray(b, np.uint8).view(ml_dtypes.float8_e4m3fn).astype(np.float64)


def setup_inputs():
    d = draw0()
    x0 = np.asarray(d['us']).astype(np.float64)
    s = (np.max(np.abs(x0), axis=(0,), keepdims=True) / 448.0).astype(np.float32)
    out = {}
    for k, v in d.items():
        if k == 'us':
            out['us_bytes'] = e4m3fn_bytes(x0 / s.astype(np.float64))
            out['us_scale'] = s
        else:
            out[k] = v
    return out


def reference(w0, coef, g, uc, us_bytes, us_scale, vc, vs):
    return core(w0, coef, g, uc, e4m3fn_values(us_bytes) * us_scale.astype(np.float64), vc, vs)

@@ -1,0 +1,254 @@
+from contextlib import ExitStack
+
+import concourse.mybir as mybir
+from concourse.masks import make_identity
+
+N = 2048
+D = 2048
+F = 128
+FLOPS = 4 * 2 * N * N * F
+
+F32 = mybir.dt.float32
+BF16 = mybir.dt.bfloat16
+U32 = mybir.dt.uint32
+U8 = mybir.dt.uint8
+FP8 = mybir.dt.float8_e4m3fn
+FP8X4 = mybir.dt.float8_e4m3fn_x4
+COPY = mybir.ActivationFunctionType.Copy
+MULT = mybir.AluOpType.mult
+ADD = mybir.AluOpType.add
+
+P = 128
+C = 4
+LEAD = 8
+LAG = 2
+
+
+def tile_fourierftgivenbases_w_kernel(tc, w0, coef, g, uc, us_bytes, us_scale, vc, vs, out):
+    nc = tc.nc
+
+    coef_v = coef.rearrange("(g m t) k -> g t m k", m=P, t=4)
+    uc_v = uc.rearrange("(g m t) k -> g t m k", m=P, t=4)
+    us_v = us_bytes.rearrange("(g m t) k -> g t m k", m=P, t=4)
+    w0_v = w0.rearrange("(g m t) f -> m g t f", m=P, t=4)
+    out_v = out.rearrange("(g m t) f -> g m t f", m=P, t=4)
+
+    seq = []
+    for i in range(8):
+        seq += [("coef", 2 * i), ("coef", 2 * i + 1), ("us", i)]
+    for i in range(8):
+        seq += [("us", 8 + i), ("uc", 2 * i), ("uc", 2 * i + 1)]
+    n_steps = len(seq)
+    where = {}
+    for s in range(n_steps):
+        where[seq[s]] = s
+
+    with ExitStack() as ctx:
+        keep = ctx.enter_context(tc.tile_pool(name="keep", bufs=1))
+        stage = ctx.enter_context(tc.tile_pool(name="stage", bufs=2))
+        psum = ctx.enter_context(tc.psum_pool(name="psum", bufs=2))
+
+        ident = keep.tile([P, P], F32, name="ident")
+        make_identity(nc, ident[:])
+
+        graw = keep.tile([P, 4, 4], BF16, name="graw")
+        gpos = keep.tile([P, 16], F32, name="gpos")
+        gneg = keep.tile([P, 16], F32, name="gneg")
+        scale_sb = keep.tile([P, N], F32, name="scale_sb", align_bytes=64)
+        vraw = keep.tile([P, C, 2, 4, F], BF16, name="vraw", align_bytes=64)
+        vgrp = keep.tile([P, C, 2 * F, 4], BF16, name="vgrp", align_bytes=64)
+        vcodes = keep.tile([P, C, 2 * F], U32, name="vcodes", align_bytes=64)
+        vscales = keep.tile([P, C, 2 * F], U8, name="vscales", align_bytes=64)
+        zcodes = keep.tile([P, C, 2 * F], U32, name="zcodes", align_bytes=64)
+        zscales = keep.tile([P, C, 2 * F], U8, name="zscales", align_bytes=64)
+        w0_sb = keep.tile([P, 4, 4, F], BF16, name="w0_sb", align_bytes=64)
+
+        raw = {}
+        codes = {}
+        scales = {}
+        grouped = {}
+        acc = {}
+        zflat = {}
+        zgrp = {}
+
+        def load(s):
+            kind, i = seq[s]
+            if kind == "us":
+                usb = stage.tile([P, N], U8, name="usb", bufs=6, align_bytes=64)
+                nc.sync.dma_start(out=usb[:], in_=us_v[i // 4, i % 4])
+                raw[s] = usb
+            else:
+                rt = stage.tile([P, N], BF16, name="raw", bufs=10, align_bytes=64)
+                src = coef_v if kind == "coef" else uc_v
+                nc.sync.dma_start(out=rt[:], in_=src[i // 4, i % 4])
+                raw[s] = rt
+
+        def product(s):
+            usp = stage.tile([P, N], BF16, name="usp", bufs=3, align_bytes=64)
+            view = raw[s][:].bitcast(FP8)
+            for h in range(2):
+                cols = slice(h * 1024, (h + 1) * 1024)
+                nc.vector.tensor_tensor(out=usp[:, cols], in0=view[:, cols], in1=scale_sb[:, cols], op=MULT)
+            raw[s] = usp
+
+        def transposes(s):
+            words = raw[s][:].bitcast(F32)
+            banks = []
+            for h in range(2):
+                xt = psum.tile([P, 2, 2, P], F32, name="xt", bufs=6)
+                for c in range(2):
+                    for u in range(2):
+                        w = 256 * (2 * h + c)
+                        nc.tensor.transpose(xt[:, c, u, :], words[:, w + u : w + 256 : 2], ident[:])
+                banks.append(xt)
+            return banks
+
+        def evacuate(s, banks):
+            gt = stage.tile([P, C, P, 4], BF16, name="grouped", bufs=4, align_bytes=64)
+            gw = gt[:].bitcast(F32)
+            for h in range(2):
+                nc.scalar.copy(out=gw[:, 2 * h : 2 * h + 2], in_=banks[h][:].rearrange("p c u r -> p c r u"))
+            grouped[s] = gt
+
+        def quantize(s):
+            kind, i = seq[s]
+            if kind == "us":
+                ct = stage.tile([P, C, P], U32, name="us_codes", bufs=16, align_bytes=64)
+                st = stage.tile([P, C, P], U8, name="us_scales", bufs=16, align_bytes=64)
+            elif kind == "coef":
+                ct = stage.tile([P, C, P], U32, name="coef_codes", bufs=5, align_bytes=64)
+                st = stage.tile([P, C, P], U8, name="coef_scales", bufs=5, align_bytes=64)
+            else:
+                ct = stage.tile([P, C, P], U32, name="uc_codes", bufs=6, align_bytes=64)
+                st = stage.tile([P, C, P], U8, name="uc_scales", bufs=6, align_bytes=64)
+            nc.vector.quantize_mx(
+                out=ct[:].rearrange("p c r -> p (c r)").bitcast(FP8X4),
+                scales=st[:].rearrange("p c r -> p (c r)"),
+                in_=grouped[s][:].rearrange("p c r t -> p (c r t)"),
+            )
+            codes[(kind, i)] = ct
+            scales[(kind, i)] = st
+
+        def mm(o, key, c, rc, rs, start, stop):
+            nc.tensor.matmul_mx(
+                out=o,
+                lhsT=codes[key][:, c, :].bitcast(FP8X4),
+                lhsT_scale=scales[key][:, c, :],
+                rhs=rc.bitcast(FP8X4),
+                rhs_scale=rs,
+                start=start,
+                stop=stop,
+            )
+
+        def stage1(pair):
+            bank = psum.tile([P, 2, 2 * F], F32, name="acc", bufs=2)
+            for j in range(2):
+                for c in range(C):
+                    mm(bank[:, j, :], ("coef", 2 * pair + j), c, vcodes[:, c, :], vscales[:, c, :], c == 0, c == C - 1)
+            acc[pair] = bank
+
+        def gain(pair):
+            gi = pair // 2
+            if pair % 2 == 0:
+                zflat[gi] = stage.tile([P, 4, 2 * F], BF16, name="zflat", bufs=2, align_bytes=64)
+            zf = zflat[gi]
+            for j in range(2):
+                i = 2 * pair + j
+                nc.scalar.activation(out=zf[:, i % 4, 0:F], in_=acc[pair][:, j, 0:F], func=COPY, scale=gpos[:, i : i + 1])
+                nc.scalar.activation(
+                    out=zf[:, i % 4, F : 2 * F], in_=acc[pair][:, j, F : 2 * F], func=COPY, scale=gneg[:, i : i + 1]
+                )
+            if pair % 2 == 1:
+                zg = stage.tile([P, 2 * F, 4], BF16, name="zgrp", bufs=2, align_bytes=64)
+                nc.scalar.copy(out=zg[:], in_=zf[:].rearrange("p t f -> p f t"))
+                zgrp[gi] = zg
+
+        def quantize_z(gi):
+            nc.vector.quantize_mx(
+                out=zcodes[:, gi, :].bitcast(FP8X4),
+                scales=zscales[:, gi, :],
+                in_=zgrp[gi][:].rearrange("p f t -> p (f t)"),
+            )
+
+        def stage2(pair):
+            bank = psum.tile([P, 2, F], F32, name="acc", bufs=2)
+            for j in range(2):
+                i = 2 * pair + j
+                for c in range(C):
+                    mm(bank[:, j, :], ("us", i), c, zcodes[:, c, F : 2 * F], zscales[:, c, F : 2 * F], c == 0, False)
+                for c in range(C):
+                    mm(bank[:, j, :], ("uc", i), c, zcodes[:, c, 0:F], zscales[:, c, 0:F], False, c == C - 1)
+            acc[("out", pair)] = bank
+
+        def epilogue(pair):
+            gi, t0 = (2 * pair) // 4, (2 * pair) % 4
+            ot = stage.tile([P, 2, F], F32, name="ot", bufs=3)
+            nc.vector.scalar_tensor_tensor(
+                out=ot[:],
+                in0=acc[("out", pair)][:],
+                scalar=0.5,
+                in1=w0_sb[:, gi, t0 : t0 + 2, :],
+                op0=MULT,
+                op1=ADD,
+            )
+            nc.sync.dma_start(out=out_v[gi, :, t0 : t0 + 2, :], in_=ot[:])
+
+        with tc.manual_schedule():
+            nc.gpsimd.dma_start(out=graw[:], in_=g.rearrange("(c p t) -> p c t", p=P, t=4))
+            load(0)
+            for k, v in ((0, vc), (1, vs)):
+                nc.sync.dma_start(out=vraw[:, :, k, :, :], in_=v.rearrange("(c p j) f -> p c j f", p=P, j=4))
+            load(1)
+            nc.sync.dma_start(out=scale_sb[:], in_=us_scale.rearrange("o k -> (o k)").partition_broadcast(P))
+            for s in range(2, LEAD):
+                load(s)
+
+            nc.vector.tensor_copy(out=gpos[:], in_=graw[:].rearrange("p c t -> p (c t)"))
+            nc.vector.tensor_scalar(
+                out=gneg[:], in0=graw[:].rearrange("p c t -> p (c t)"), scalar1=-1.0, scalar2=None, op0=MULT
+            )
+            nc.vector.tensor_copy(
+                out=vgrp[:, :, 0:F, :], in_=vraw[:, :, 0, :, :].rearrange("p c j f -> p c f j")
+            )
+            nc.scalar.copy(
+                out=vgrp[:, :, F : 2 * F, :], in_=vraw[:, :, 1, :, :].rearrange("p c j f -> p c f j")
+            )
+
+            pend1 = list(range(8))
+            pend2 = list(range(8))
+            later = []
+            for s in range(n_steps + LAG + 2):
+                if s + LEAD < n_steps:
+                    load(s + LEAD)
+                if s == 20:
+                    nc.sync.dma_start(out=w0_sb[:], in_=w0_v)
+                if s + 2 < n_steps and seq[s + 2][0] == "us":
+                    product(s + 2)
+                if s == 1:
+                    nc.vector.quantize_mx(
+                        out=vcodes[:].rearrange("p c f -> p (c f)").bitcast(FP8X4),
+                        scales=vscales[:].rearrange("p c f -> p (c f)"),
+                        in_=vgrp[:].rearrange("p c f j -> p (c f j)"),
+                    )
+                for fn, arg in later:
+                    fn(arg)
+                later = []
+                if s < n_steps:
+                    banks = transposes(s)
+                    evacuate(s, banks)
+                if 1 <= s <= n_steps:
+                    quantize(s - 1)
+                while pend1 and where[("coef", 2 * pend1[0] + 1)] <= s - LAG:
+                    pair = pend1.pop(0)
+                    stage1(pair)
+                    gain(pair)
+                    if pair % 2 == 1:
+                        later.append((quantize_z, pair // 2))
+                while (
+                    pend2
+                    and s >= 28
+                    and max(where[("uc", 2 * pend2[0] + 1)], where[("us", 2 * pend2[0] + 1)]) <= s - LAG
+                ):
+                    pair = pend2.pop(0)
+                    stage2(pair)
+                    later.append((epilogue, pair))

@@ -20,8 +20,8 @@ ADD = mybir.AluOpType.add
 
 P = 128
 C = 4
-LEAD = 8
-LAG = 2
+KINDS = "ccuccuccuccuUuUUuUUuUUuU"
+LEAD = 5
 
 
 def tile_fourierftgivenbases_w_kernel(tc, w0, coef, g, uc, us_bytes, us_scale, vc, vs, out):
@@ -33,15 +33,25 @@ def tile_fourierftgivenbases_w_kernel(tc, w0, coef, g, uc, us_bytes, us_scale, v
     w0_v = w0.rearrange("(g m t) f -> m g t f", m=P, t=4)
     out_v = out.rearrange("(g m t) f -> g m t f", m=P, t=4)
 
-    seq = []
-    for i in range(8):
-        seq += [("coef", 2 * i), ("coef", 2 * i + 1), ("us", i)]
-    for i in range(8):
-        seq += [("us", 8 + i), ("uc", 2 * i), ("uc", 2 * i + 1)]
-    n_steps = len(seq)
-    where = {}
-    for s in range(n_steps):
-        where[seq[s]] = s
+    pairs = []
+    count = {"c": 0, "u": 0, "U": 0}
+    for kind in KINDS:
+        pairs.append((kind, count[kind]))
+        count[kind] += 1
+    n_pairs = len(pairs)
+    at = {}
+    for s in range(n_pairs):
+        at[pairs[s]] = s
+
+    product_step = {}
+    for k in range(16):
+        product_step[k] = min(at[("u", k // 2)] - 1, (11 * k) // 8)
+    load_step = {}
+    for s in range(n_pairs):
+        kind, q = pairs[s]
+        for j in range(2):
+            load_step[(kind, 2 * q + j)] = (product_step[2 * q + j] - 0.5) if kind == "u" else s
+    order = sorted(load_step, key=lambda key: (load_step[key], key[1]))
 
     with ExitStack() as ctx:
         keep = ctx.enter_context(tc.tile_pool(name="keep", bufs=1))
@@ -71,94 +81,84 @@ def tile_fourierftgivenbases_w_kernel(tc, w0, coef, g, uc, us_bytes, us_scale, v
         zflat = {}
         zgrp = {}
 
-        def load(s):
-            kind, i = seq[s]
-            if kind == "us":
+        def load(key):
+            kind, i = key
+            if kind == "u":
                 usb = stage.tile([P, N], U8, name="usb", bufs=6, align_bytes=64)
                 nc.sync.dma_start(out=usb[:], in_=us_v[i // 4, i % 4])
-                raw[s] = usb
+                raw[key] = usb
             else:
                 rt = stage.tile([P, N], BF16, name="raw", bufs=10, align_bytes=64)
-                src = coef_v if kind == "coef" else uc_v
+                src = coef_v if kind == "c" else uc_v
                 nc.sync.dma_start(out=rt[:], in_=src[i // 4, i % 4])
-                raw[s] = rt
+                raw[key] = rt
 
-        def product(s):
-            usp = stage.tile([P, N], BF16, name="usp", bufs=3, align_bytes=64)
-            view = raw[s][:].bitcast(FP8)
-            for h in range(2):
-                cols = slice(h * 1024, (h + 1) * 1024)
-                nc.vector.tensor_tensor(out=usp[:, cols], in0=view[:, cols], in1=scale_sb[:, cols], op=MULT)
-            raw[s] = usp
+        def product(k):
+            usp = stage.tile([P, N], BF16, name="usp", bufs=5, align_bytes=64)
+            nc.vector.tensor_tensor(out=usp[:], in0=raw[("u", k)][:].bitcast(FP8), in1=scale_sb[:], op=MULT)
+            raw[("u", k)] = usp
 
-        def transposes(s):
-            words = raw[s][:].bitcast(F32)
-            banks = []
-            for h in range(2):
-                xt = psum.tile([P, 2, 2, P], F32, name="xt", bufs=6)
-                for c in range(2):
-                    for u in range(2):
-                        w = 256 * (2 * h + c)
-                        nc.tensor.transpose(xt[:, c, u, :], words[:, w + u : w + 256 : 2], ident[:])
-                banks.append(xt)
-            return banks
-
-        def evacuate(s, banks):
-            gt = stage.tile([P, C, P, 4], BF16, name="grouped", bufs=4, align_bytes=64)
+        def turn(s):
+            kind, q = pairs[s]
+            gt = stage.tile([P, 2, C, P, 4], BF16, name="grouped", bufs=3, align_bytes=64)
             gw = gt[:].bitcast(F32)
-            for h in range(2):
-                nc.scalar.copy(out=gw[:, 2 * h : 2 * h + 2], in_=banks[h][:].rearrange("p c u r -> p c r u"))
+            for j in range(2):
+                words = raw[(kind, 2 * q + j)][:].bitcast(F32)
+                for h in range(2):
+                    xt = psum.tile([P, 2, 2, P], F32, name="xt", bufs=6)
+                    for c in range(2):
+                        for u in range(2):
+                            w = 256 * (2 * h + c)
+                            nc.tensor.transpose(xt[:, c, u, :], words[:, w + u : w + 256 : 2], ident[:])
+                    nc.scalar.copy(out=gw[:, j, 2 * h : 2 * h + 2], in_=xt[:].rearrange("p c u r -> p c r u"))
             grouped[s] = gt
 
         def quantize(s):
-            kind, i = seq[s]
-            if kind == "us":
-                ct = stage.tile([P, C, P], U32, name="us_codes", bufs=16, align_bytes=64)
-                st = stage.tile([P, C, P], U8, name="us_scales", bufs=16, align_bytes=64)
-            elif kind == "coef":
-                ct = stage.tile([P, C, P], U32, name="coef_codes", bufs=5, align_bytes=64)
-                st = stage.tile([P, C, P], U8, name="coef_scales", bufs=5, align_bytes=64)
+            kind, q = pairs[s]
+            if kind == "u":
+                ct = stage.tile([P, 2, C, P], U32, name="us_codes", bufs=8, align_bytes=64)
+                st = stage.tile([P, 2, C, P], U8, name="us_scales", bufs=8, align_bytes=64)
+            elif kind == "c":
+                ct = stage.tile([P, 2, C, P], U32, name="coef_codes", bufs=3, align_bytes=64)
+                st = stage.tile([P, 2, C, P], U8, name="coef_scales", bufs=3, align_bytes=64)
             else:
-                ct = stage.tile([P, C, P], U32, name="uc_codes", bufs=6, align_bytes=64)
-                st = stage.tile([P, C, P], U8, name="uc_scales", bufs=6, align_bytes=64)
+                ct = stage.tile([P, 2, C, P], U32, name="uc_codes", bufs=4, align_bytes=64)
+                st = stage.tile([P, 2, C, P], U8, name="uc_scales", bufs=4, align_bytes=64)
             nc.vector.quantize_mx(
-                out=ct[:].rearrange("p c r -> p (c r)").bitcast(FP8X4),
-                scales=st[:].rearrange("p c r -> p (c r)"),
-                in_=grouped[s][:].rearrange("p c r t -> p (c r t)"),
+                out=ct[:].rearrange("p j c r -> p (j c r)").bitcast(FP8X4),
+                scales=st[:].rearrange("p j c r -> p (j c r)"),
+                in_=grouped[s][:].rearrange("p j c r t -> p (j c r t)"),
             )
-            codes[(kind, i)] = ct
-            scales[(kind, i)] = st
+            codes[(kind, q)] = ct
+            scales[(kind, q)] = st
 
-        def mm(o, key, c, rc, rs, start, stop):
+        def mm(o, kind, i, c, rc, rs, start, stop):
             nc.tensor.matmul_mx(
                 out=o,
-                lhsT=codes[key][:, c, :].bitcast(FP8X4),
-                lhsT_scale=scales[key][:, c, :],
+                lhsT=codes[(kind, i // 2)][:, i % 2, c, :].bitcast(FP8X4),
+                lhsT_scale=scales[(kind, i // 2)][:, i % 2, c, :],
                 rhs=rc.bitcast(FP8X4),
                 rhs_scale=rs,
                 start=start,
                 stop=stop,
             )
 
-        def stage1(pair):
-            bank = psum.tile([P, 2, 2 * F], F32, name="acc", bufs=2)
-            for j in range(2):
-                for c in range(C):
-                    mm(bank[:, j, :], ("coef", 2 * pair + j), c, vcodes[:, c, :], vscales[:, c, :], c == 0, c == C - 1)
-            acc[pair] = bank
+        def stage1(i):
+            bank = psum.tile([P, 2 * F], F32, name="acc", bufs=2)
+            for c in range(C):
+                mm(bank[:], "c", i, c, vcodes[:, c, :], vscales[:, c, :], c == 0, c == C - 1)
+            acc[i] = bank
 
-        def gain(pair):
-            gi = pair // 2
-            if pair % 2 == 0:
+        def gain(i):
+            gi = i // 4
+            if i % 4 == 0:
                 zflat[gi] = stage.tile([P, 4, 2 * F], BF16, name="zflat", bufs=2, align_bytes=64)
             zf = zflat[gi]
-            for j in range(2):
-                i = 2 * pair + j
-                nc.scalar.activation(out=zf[:, i % 4, 0:F], in_=acc[pair][:, j, 0:F], func=COPY, scale=gpos[:, i : i + 1])
-                nc.scalar.activation(
-                    out=zf[:, i % 4, F : 2 * F], in_=acc[pair][:, j, F : 2 * F], func=COPY, scale=gneg[:, i : i + 1]
-                )
-            if pair % 2 == 1:
+            nc.scalar.activation(out=zf[:, i % 4, 0:F], in_=acc[i][:, 0:F], func=COPY, scale=gpos[:, i : i + 1])
+            nc.scalar.activation(
+                out=zf[:, i % 4, F : 2 * F], in_=acc[i][:, F : 2 * F], func=COPY, scale=gneg[:, i : i + 1]
+            )
+            if i % 4 == 3:
                 zg = stage.tile([P, 2 * F, 4], BF16, name="zgrp", bufs=2, align_bytes=64)
                 nc.scalar.copy(out=zg[:], in_=zf[:].rearrange("p t f -> p f t"))
                 zgrp[gi] = zg
@@ -170,22 +170,21 @@ def tile_fourierftgivenbases_w_kernel(tc, w0, coef, g, uc, us_bytes, us_scale, v
                 in_=zgrp[gi][:].rearrange("p f t -> p (f t)"),
             )
 
-        def stage2(pair):
+        def stage2(q):
             bank = psum.tile([P, 2, F], F32, name="acc", bufs=2)
             for j in range(2):
-                i = 2 * pair + j
                 for c in range(C):
-                    mm(bank[:, j, :], ("us", i), c, zcodes[:, c, F : 2 * F], zscales[:, c, F : 2 * F], c == 0, False)
+                    mm(bank[:, j, :], "u", 2 * q + j, c, zcodes[:, c, F : 2 * F], zscales[:, c, F : 2 * F], c == 0, False)
                 for c in range(C):
-                    mm(bank[:, j, :], ("uc", i), c, zcodes[:, c, 0:F], zscales[:, c, 0:F], False, c == C - 1)
-            acc[("out", pair)] = bank
+                    mm(bank[:, j, :], "U", 2 * q + j, c, zcodes[:, c, 0:F], zscales[:, c, 0:F], False, c == C - 1)
+            acc[("out", q)] = bank
 
-        def epilogue(pair):
-            gi, t0 = (2 * pair) // 4, (2 * pair) % 4
-            ot = stage.tile([P, 2, F], F32, name="ot", bufs=3)
+        def epilogue(q):
+            gi, t0 = q // 2, 2 * (q % 2)
+            ot = stage.tile([P, 2, F], F32, name="ot", bufs=4)
             nc.vector.scalar_tensor_tensor(
                 out=ot[:],
-                in0=acc[("out", pair)][:],
+                in0=acc[("out", q)][:],
                 scalar=0.5,
                 in1=w0_sb[:, gi, t0 : t0 + 2, :],
                 op0=MULT,
@@ -194,61 +193,67 @@ def tile_fourierftgivenbases_w_kernel(tc, w0, coef, g, uc, us_bytes, us_scale, v
             nc.sync.dma_start(out=out_v[gi, :, t0 : t0 + 2, :], in_=ot[:])
 
         with tc.manual_schedule():
-            nc.gpsimd.dma_start(out=graw[:], in_=g.rearrange("(c p t) -> p c t", p=P, t=4))
-            load(0)
+            todo = list(order)
+            load(todo.pop(0))
+            load(todo.pop(0))
+            nc.sync.dma_start(out=scale_sb[:], in_=us_scale.rearrange("o k -> (o k)").partition_broadcast(P))
+            load(todo.pop(0))
+            load(todo.pop(0))
             for k, v in ((0, vc), (1, vs)):
                 nc.sync.dma_start(out=vraw[:, :, k, :, :], in_=v.rearrange("(c p j) f -> p c j f", p=P, j=4))
-            load(1)
-            nc.sync.dma_start(out=scale_sb[:], in_=us_scale.rearrange("o k -> (o k)").partition_broadcast(P))
-            for s in range(2, LEAD):
-                load(s)
+            nc.sync.dma_start(out=graw[:], in_=g.rearrange("(c p t) -> p c t", p=P, t=4))
 
-            nc.vector.tensor_copy(out=gpos[:], in_=graw[:].rearrange("p c t -> p (c t)"))
-            nc.vector.tensor_scalar(
-                out=gneg[:], in0=graw[:].rearrange("p c t -> p (c t)"), scalar1=-1.0, scalar2=None, op0=MULT
-            )
-            nc.vector.tensor_copy(
-                out=vgrp[:, :, 0:F, :], in_=vraw[:, :, 0, :, :].rearrange("p c j f -> p c f j")
-            )
-            nc.scalar.copy(
-                out=vgrp[:, :, F : 2 * F, :], in_=vraw[:, :, 1, :, :].rearrange("p c j f -> p c f j")
-            )
-
-            pend1 = list(range(8))
-            pend2 = list(range(8))
+            units1 = []
+            units2 = []
             later = []
-            for s in range(n_steps + LAG + 2):
-                if s + LEAD < n_steps:
-                    load(s + LEAD)
-                if s == 20:
+            done1 = 0
+            for s in range(n_pairs + 3):
+                while todo and load_step[todo[0]] <= s + LEAD:
+                    load(todo.pop(0))
+                if s == 10:
                     nc.sync.dma_start(out=w0_sb[:], in_=w0_v)
-                if s + 2 < n_steps and seq[s + 2][0] == "us":
-                    product(s + 2)
+                for k in range(16):
+                    if product_step[k] == s:
+                        product(k)
+                for fn, arg in later:
+                    fn(arg)
+                later = []
+                if s < n_pairs:
+                    turn(s)
+                if 1 <= s <= n_pairs:
+                    quantize(s - 1)
                 if s == 1:
+                    nc.vector.tensor_copy(
+                        out=vgrp[:, :, 0:F, :], in_=vraw[:, :, 0, :, :].rearrange("p c j f -> p c f j")
+                    )
+                    nc.scalar.copy(
+                        out=vgrp[:, :, F : 2 * F, :], in_=vraw[:, :, 1, :, :].rearrange("p c j f -> p c f j")
+                    )
+                    nc.vector.tensor_copy(out=gpos[:], in_=graw[:].rearrange("p c t -> p (c t)"))
+                    nc.vector.tensor_scalar(
+                        out=gneg[:], in0=graw[:].rearrange("p c t -> p (c t)"), scalar1=-1.0, scalar2=None, op0=MULT
+                    )
+                if s == 2:
                     nc.vector.quantize_mx(
                         out=vcodes[:].rearrange("p c f -> p (c f)").bitcast(FP8X4),
                         scales=vscales[:].rearrange("p c f -> p (c f)"),
                         in_=vgrp[:].rearrange("p c f j -> p (c f j)"),
                     )
-                for fn, arg in later:
-                    fn(arg)
-                later = []
-                if s < n_steps:
-                    banks = transposes(s)
-                    evacuate(s, banks)
-                if 1 <= s <= n_steps:
-                    quantize(s - 1)
-                while pend1 and where[("coef", 2 * pend1[0] + 1)] <= s - LAG:
-                    pair = pend1.pop(0)
-                    stage1(pair)
-                    gain(pair)
-                    if pair % 2 == 1:
-                        later.append((quantize_z, pair // 2))
-                while (
-                    pend2
-                    and s >= 28
-                    and max(where[("uc", 2 * pend2[0] + 1)], where[("us", 2 * pend2[0] + 1)]) <= s - LAG
-                ):
-                    pair = pend2.pop(0)
-                    stage2(pair)
-                    later.append((epilogue, pair))
+                if s >= 2 and s - 2 < n_pairs and pairs[s - 2][0] == "c":
+                    units1 += [2 * pairs[s - 2][1], 2 * pairs[s - 2][1] + 1]
+                if s >= 2 and s - 2 < n_pairs and pairs[s - 2][0] == "U":
+                    units2 += [pairs[s - 2][1]]
+                n1 = 0 if s < 3 else len(units1) if (len(units1) < 2 or s >= at[("c", 7)] + 2) else (2 if len(units1) > 2 else 1)
+                for i in units1[:n1]:
+                    stage1(i)
+                    gain(i)
+                    done1 += 1
+                    if i % 4 == 3:
+                        later.append((quantize_z, i // 4))
+                units1 = units1[n1:]
+                if n1 == 0 and s >= at[("c", 7)] + 4:
+                    n2 = len(units2) if s >= n_pairs else 1
+                    for i in units2[:n2]:
+                        stage2(i)
+                        later.append((epilogue, i))
+                    units2 = units2[n2:]

from contextlib import ExitStack

import concourse.mybir as mybir
from concourse.masks import make_identity

N = 2048
D = 2048
F = 128
FLOPS = 4 * 2 * N * N * F

F32 = mybir.dt.float32
BF16 = mybir.dt.bfloat16
U32 = mybir.dt.uint32
U8 = mybir.dt.uint8
FP8 = mybir.dt.float8_e4m3fn
FP8X4 = mybir.dt.float8_e4m3fn_x4
COPY = mybir.ActivationFunctionType.Copy
MULT = mybir.AluOpType.mult
ADD = mybir.AluOpType.add

P = 128
C = 4
KINDS = "ccuccuccuccuUuUUuUUuUUuU"
LEAD = 5


def tile_fourierftgivenbases_w_kernel(tc, w0, coef, g, uc, us_bytes, us_scale, vc, vs, out):
    nc = tc.nc

    coef_v = coef.rearrange("(g m t) k -> g t m k", m=P, t=4)
    uc_v = uc.rearrange("(g m t) k -> g t m k", m=P, t=4)
    us_v = us_bytes.rearrange("(g m t) k -> g t m k", m=P, t=4)
    w0_v = w0.rearrange("(g m t) f -> m g t f", m=P, t=4)
    out_v = out.rearrange("(g m t) f -> g m t f", m=P, t=4)

    pairs = []
    count = {"c": 0, "u": 0, "U": 0}
    for kind in KINDS:
        pairs.append((kind, count[kind]))
        count[kind] += 1
    n_pairs = len(pairs)
    at = {}
    for s in range(n_pairs):
        at[pairs[s]] = s

    product_step = {}
    for k in range(16):
        product_step[k] = min(at[("u", k // 2)] - 1, (11 * k) // 8)
    load_step = {}
    for s in range(n_pairs):
        kind, q = pairs[s]
        for j in range(2):
            load_step[(kind, 2 * q + j)] = (product_step[2 * q + j] - 0.5) if kind == "u" else s
    order = sorted(load_step, key=lambda key: (load_step[key], key[1]))

    with ExitStack() as ctx:
        keep = ctx.enter_context(tc.tile_pool(name="keep", bufs=1))
        stage = ctx.enter_context(tc.tile_pool(name="stage", bufs=2))
        psum = ctx.enter_context(tc.psum_pool(name="psum", bufs=2))

        ident = keep.tile([P, P], F32, name="ident")
        make_identity(nc, ident[:])

        graw = keep.tile([P, 4, 4], BF16, name="graw")
        gpos = keep.tile([P, 16], F32, name="gpos")
        gneg = keep.tile([P, 16], F32, name="gneg")
        scale_sb = keep.tile([P, N], F32, name="scale_sb", align_bytes=64)
        vraw = keep.tile([P, C, 2, 4, F], BF16, name="vraw", align_bytes=64)
        vgrp = keep.tile([P, C, 2 * F, 4], BF16, name="vgrp", align_bytes=64)
        vcodes = keep.tile([P, C, 2 * F], U32, name="vcodes", align_bytes=64)
        vscales = keep.tile([P, C, 2 * F], U8, name="vscales", align_bytes=64)
        zcodes = keep.tile([P, C, 2 * F], U32, name="zcodes", align_bytes=64)
        zscales = keep.tile([P, C, 2 * F], U8, name="zscales", align_bytes=64)
        w0_sb = keep.tile([P, 4, 4, F], BF16, name="w0_sb", align_bytes=64)

        raw = {}
        codes = {}
        scales = {}
        grouped = {}
        acc = {}
        zflat = {}
        zgrp = {}

        def load(key):
            kind, i = key
            if kind == "u":
                usb = stage.tile([P, N], U8, name="usb", bufs=6, align_bytes=64)
                nc.sync.dma_start(out=usb[:], in_=us_v[i // 4, i % 4])
                raw[key] = usb
            else:
                rt = stage.tile([P, N], BF16, name="raw", bufs=10, align_bytes=64)
                src = coef_v if kind == "c" else uc_v
                nc.sync.dma_start(out=rt[:], in_=src[i // 4, i % 4])
                raw[key] = rt

        def product(k):
            usp = stage.tile([P, N], BF16, name="usp", bufs=5, align_bytes=64)
            nc.vector.tensor_tensor(out=usp[:], in0=raw[("u", k)][:].bitcast(FP8), in1=scale_sb[:], op=MULT)
            raw[("u", k)] = usp

        def turn(s):
            kind, q = pairs[s]
            gt = stage.tile([P, 2, C, P, 4], BF16, name="grouped", bufs=3, align_bytes=64)
            gw = gt[:].bitcast(F32)
            for j in range(2):
                words = raw[(kind, 2 * q + j)][:].bitcast(F32)
                for h in range(2):
                    xt = psum.tile([P, 2, 2, P], F32, name="xt", bufs=6)
                    for c in range(2):
                        for u in range(2):
                            w = 256 * (2 * h + c)
                            nc.tensor.transpose(xt[:, c, u, :], words[:, w + u : w + 256 : 2], ident[:])
                    nc.scalar.copy(out=gw[:, j, 2 * h : 2 * h + 2], in_=xt[:].rearrange("p c u r -> p c r u"))
            grouped[s] = gt

        def quantize(s):
            kind, q = pairs[s]
            if kind == "u":
                ct = stage.tile([P, 2, C, P], U32, name="us_codes", bufs=8, align_bytes=64)
                st = stage.tile([P, 2, C, P], U8, name="us_scales", bufs=8, align_bytes=64)
            elif kind == "c":
                ct = stage.tile([P, 2, C, P], U32, name="coef_codes", bufs=3, align_bytes=64)
                st = stage.tile([P, 2, C, P], U8, name="coef_scales", bufs=3, align_bytes=64)
            else:
                ct = stage.tile([P, 2, C, P], U32, name="uc_codes", bufs=4, align_bytes=64)
                st = stage.tile([P, 2, C, P], U8, name="uc_scales", bufs=4, align_bytes=64)
            nc.vector.quantize_mx(
                out=ct[:].rearrange("p j c r -> p (j c r)").bitcast(FP8X4),
                scales=st[:].rearrange("p j c r -> p (j c r)"),
                in_=grouped[s][:].rearrange("p j c r t -> p (j c r t)"),
            )
            codes[(kind, q)] = ct
            scales[(kind, q)] = st

        def mm(o, kind, i, c, rc, rs, start, stop):
            nc.tensor.matmul_mx(
                out=o,
                lhsT=codes[(kind, i // 2)][:, i % 2, c, :].bitcast(FP8X4),
                lhsT_scale=scales[(kind, i // 2)][:, i % 2, c, :],
                rhs=rc.bitcast(FP8X4),
                rhs_scale=rs,
                start=start,
                stop=stop,
            )

        def stage1(i):
            bank = psum.tile([P, 2 * F], F32, name="acc", bufs=2)
            for c in range(C):
                mm(bank[:], "c", i, c, vcodes[:, c, :], vscales[:, c, :], c == 0, c == C - 1)
            acc[i] = bank

        def gain(i):
            gi = i // 4
            if i % 4 == 0:
                zflat[gi] = stage.tile([P, 4, 2 * F], BF16, name="zflat", bufs=2, align_bytes=64)
            zf = zflat[gi]
            nc.scalar.activation(out=zf[:, i % 4, 0:F], in_=acc[i][:, 0:F], func=COPY, scale=gpos[:, i : i + 1])
            nc.scalar.activation(
                out=zf[:, i % 4, F : 2 * F], in_=acc[i][:, F : 2 * F], func=COPY, scale=gneg[:, i : i + 1]
            )
            if i % 4 == 3:
                zg = stage.tile([P, 2 * F, 4], BF16, name="zgrp", bufs=2, align_bytes=64)
                nc.scalar.copy(out=zg[:], in_=zf[:].rearrange("p t f -> p f t"))
                zgrp[gi] = zg

        def quantize_z(gi):
            nc.vector.quantize_mx(
                out=zcodes[:, gi, :].bitcast(FP8X4),
                scales=zscales[:, gi, :],
                in_=zgrp[gi][:].rearrange("p f t -> p (f t)"),
            )

        def stage2(q):
            bank = psum.tile([P, 2, F], F32, name="acc", bufs=2)
            for j in range(2):
                for c in range(C):
                    mm(bank[:, j, :], "u", 2 * q + j, c, zcodes[:, c, F : 2 * F], zscales[:, c, F : 2 * F], c == 0, False)
                for c in range(C):
                    mm(bank[:, j, :], "U", 2 * q + j, c, zcodes[:, c, 0:F], zscales[:, c, 0:F], False, c == C - 1)
            acc[("out", q)] = bank

        def epilogue(q):
            gi, t0 = q // 2, 2 * (q % 2)
            ot = stage.tile([P, 2, F], F32, name="ot", bufs=4)
            nc.vector.scalar_tensor_tensor(
                out=ot[:],
                in0=acc[("out", q)][:],
                scalar=0.5,
                in1=w0_sb[:, gi, t0 : t0 + 2, :],
                op0=MULT,
                op1=ADD,
            )
            nc.sync.dma_start(out=out_v[gi, :, t0 : t0 + 2, :], in_=ot[:])

        with tc.manual_schedule():
            todo = list(order)
            load(todo.pop(0))
            load(todo.pop(0))
            nc.sync.dma_start(out=scale_sb[:], in_=us_scale.rearrange("o k -> (o k)").partition_broadcast(P))
            load(todo.pop(0))
            load(todo.pop(0))
            for k, v in ((0, vc), (1, vs)):
                nc.sync.dma_start(out=vraw[:, :, k, :, :], in_=v.rearrange("(c p j) f -> p c j f", p=P, j=4))
            nc.sync.dma_start(out=graw[:], in_=g.rearrange("(c p t) -> p c t", p=P, t=4))

            units1 = []
            units2 = []
            later = []
            done1 = 0
            for s in range(n_pairs + 3):
                while todo and load_step[todo[0]] <= s + LEAD:
                    load(todo.pop(0))
                if s == 10:
                    nc.sync.dma_start(out=w0_sb[:], in_=w0_v)
                for k in range(16):
                    if product_step[k] == s:
                        product(k)
                for fn, arg in later:
                    fn(arg)
                later = []
                if s < n_pairs:
                    turn(s)
                if 1 <= s <= n_pairs:
                    quantize(s - 1)
                if s == 1:
                    nc.vector.tensor_copy(
                        out=vgrp[:, :, 0:F, :], in_=vraw[:, :, 0, :, :].rearrange("p c j f -> p c f j")
                    )
                    nc.scalar.copy(
                        out=vgrp[:, :, F : 2 * F, :], in_=vraw[:, :, 1, :, :].rearrange("p c j f -> p c f j")
                    )
                    nc.vector.tensor_copy(out=gpos[:], in_=graw[:].rearrange("p c t -> p (c t)"))
                    nc.vector.tensor_scalar(
                        out=gneg[:], in0=graw[:].rearrange("p c t -> p (c t)"), scalar1=-1.0, scalar2=None, op0=MULT
                    )
                if s == 2:
                    nc.vector.quantize_mx(
                        out=vcodes[:].rearrange("p c f -> p (c f)").bitcast(FP8X4),
                        scales=vscales[:].rearrange("p c f -> p (c f)"),
                        in_=vgrp[:].rearrange("p c f j -> p (c f j)"),
                    )
                if s >= 2 and s - 2 < n_pairs and pairs[s - 2][0] == "c":
                    units1 += [2 * pairs[s - 2][1], 2 * pairs[s - 2][1] + 1]
                if s >= 2 and s - 2 < n_pairs and pairs[s - 2][0] == "U":
                    units2 += [pairs[s - 2][1]]
                n1 = 0 if s < 3 else len(units1) if (len(units1) < 2 or s >= at[("c", 7)] + 2) else (2 if len(units1) > 2 else 1)
                for i in units1[:n1]:
                    stage1(i)
                    gain(i)
                    done1 += 1
                    if i % 4 == 3:
                        later.append((quantize_z, i // 4))
                units1 = units1[n1:]
                if n1 == 0 and s >= at[("c", 7)] + 4:
                    n2 = len(units2) if s >= n_pairs else 1
                    for i in units2[:n2]:
                        stage2(i)
                        later.append((epilogue, i))
                    units2 = units2[n2:]
